import numpy as np
import ml_dtypes


def mxq(x, axis, fmt="e4m3"):
    dtype, down = {"e4m3": (ml_dtypes.float8_e4m3fn, 7), "e5m2": (ml_dtypes.float8_e5m2, 14)}[fmt]
    v = np.moveaxis(np.asarray(x, np.float32).astype(ml_dtypes.bfloat16).astype(np.float64), axis, -1)
    blocks = v.reshape(v.shape[:-1] + (-1, 32))
    amax = np.abs(blocks).max(-1, keepdims=True)
    byte = np.maximum(np.where(amax > 0, np.frexp(amax)[1] - 1 + 127, 0) - down, 1)
    scale = np.exp2(byte - 127.0)
    codes = (blocks / scale).astype(np.float32).astype(dtype).astype(np.float64)
    return np.moveaxis((codes * scale).reshape(v.shape), -1, axis)


WIDE = False


def mx_kscale(k):
    if not WIDE:
        return np.ones(k)
    levels = np.array([24, -24, 12, -12, 0])
    if k % 512:
        return np.exp2(np.random.permutation(np.resize(levels, k // 32))).repeat(32)
    a = np.empty((k // 512, 16))
    for p in range(k // 512):
        a[p, :8] = np.random.permutation(np.resize(levels, 8))
        for g in range(8):
            far = levels[np.abs(levels - a[p, g]) >= 10]
            a[p, g + 8] = far[np.random.randint(len(far))]
    return np.exp2(a.ravel()).repeat(32)


def f64(x):
    return np.asarray(x).astype(np.float64)


def striped(idx):
    return np.tile(idx.reshape(-1, 16).T, (8, 1)).astype(np.uint16)


def unstriped(offs):
    return offs[:16].T.reshape(-1).astype(np.int64)


E2M1 = np.array([0.0, 0.5, 1.0, 1.5, 2.0, 3.0, 4.0, 6.0, -0.0, -0.5, -1.0, -1.5, -2.0, -3.0, -4.0, -6.0])


def pack_weight(w, fmt):
    k, n = w.shape
    w = f64(np.asarray(w, np.float32).astype(ml_dtypes.bfloat16)).reshape(k // 32, 32, n)
    amax = np.abs(w).max(1)
    if fmt == "e4m3":
        byte = np.frexp(amax)[1] - 1 + 127 - 7
    else:
        mant, ex = np.frexp(amax / 6.0)
        byte = np.where(mant > 0.5, ex, ex - 1) + 127
    byte = np.clip(np.where(amax > 0, byte, 1), 1, 254)
    scaled = (w * np.exp2(127.0 - byte)[:, None, :]).reshape(k, n).astype(np.float32)
    by_word = np.ascontiguousarray(scaled.reshape(k // 512, 128, 4, n).transpose(0, 1, 3, 2))
    if fmt == "e4m3":
        words = by_word.astype(ml_dtypes.float8_e4m3fn).view(np.uint8)
    else:
        c = by_word.astype(ml_dtypes.float4_e2m1fn).view(np.uint8) & 0xF
        words = (c[..., 0::2] | (c[..., 1::2] << 4)).reshape(k // 512, 128, 2 * n)
    return np.ascontiguousarray(words), np.ascontiguousarray(byte.astype(np.uint8).reshape(k // 512, 16, n))


def unpack_weight(words, scales, fmt):
    g, _, n = scales.shape
    words = np.ascontiguousarray(words).reshape(g, 128, n, -1)
    if fmt == "e4m3":
        vals = words.view(ml_dtypes.float8_e4m3fn).astype(np.float64)
    else:
        nib = np.empty((g, 128, n, 4), np.uint8)
        nib[..., 0::2] = words & 0xF
        nib[..., 1::2] = words >> 4
        vals = E2M1[nib]
    vals = vals * np.repeat(np.exp2(scales.astype(np.float64) - 127.0), 8, axis=1)[..., None]
    return vals.transpose(0, 1, 3, 2).reshape(g * 512, n)


def sigm(f):
    return 1.0 / (1.0 + np.exp(-np.maximum(f, -700.0)))


K, M, N, T, J = 512, 512, 512, 2048, 1024


def setup_inputs():
    n = np.random.standard_normal
    s = mx_kscale(K)[:, None]
    s2 = mx_kscale(M)[:, None]
    h = np.tanh(n((N, T)))
    p_tab = pack_weight(h * s2, "e4m3")
    p_wz = pack_weight(n((K, N)) / np.sqrt(K) / s, "e4m3")
    p_uz = pack_weight(n((M, N)) / np.sqrt(M) / s2, "e4m3")
    p_wn = pack_weight(n((K, N)) / np.sqrt(K) / s, "e4m3")
    p_un = pack_weight(n((M, N)) / np.sqrt(M) / s2, "e4m3")
    return {
        "x": (n((K, J)) * s).astype(np.float32),
        "tab_words": p_tab[0],
        "tab_scales": p_tab[1],
        "wz_words": p_wz[0],
        "wz_scales": p_wz[1],
        "uz_words": p_uz[0],
        "uz_scales": p_uz[1],
        "wn_words": p_wn[0],
        "wn_scales": p_wn[1],
        "un_words": p_un[0],
        "un_scales": p_un[1],
        "bz": (0.3 * n(N)).astype(np.float32),
        "bn": (0.3 * n(N)).astype(np.float32),
        "hT": (h).astype(np.float32),
        "wgo": np.tile(np.random.uniform(0.5, 2.0, J), (128, 1)).astype(np.float32),
        "offs": striped(np.random.permutation(T)[:J]),
    }


def reference(x, tab_words, tab_scales, wz_words, wz_scales, uz_words, uz_scales, wn_words, wn_scales, un_words, un_scales, bz, bn, hT, wgo, offs):
    idx = unstriped(offs)
    x_ = mxq(f64(x), 0, "e4m3")
    tab_ = unpack_weight(tab_words, tab_scales, "e4m3")[:, idx]
    wz_ = unpack_weight(wz_words, wz_scales, "e4m3")
    uz_ = unpack_weight(uz_words, uz_scales, "e4m3")
    wn_ = unpack_weight(wn_words, wn_scales, "e4m3")
    un_ = unpack_weight(un_words, un_scales, "e4m3")
    sz = wz_.T @ x_ + uz_.T @ tab_
    z = sigm(sz + f64(bz)[:, None])
    sn = wn_.T @ x_ + un_.T @ tab_
    cd = np.tanh(sn + f64(bn)[:, None])
    out = np.zeros((N, T))
    out[:, idx] = f64(wgo)[0] * (f64(hT)[:, idx] + z * (cd - f64(hT)[:, idx]))
    return out

@@ -1,0 +1,200 @@
+from contextlib import ExitStack
+
+import concourse.mybir as mybir
+from concourse.masks import make_identity
+
+K, M, N, T, J = 512, 512, 512, 2048, 1024
+FLOPS = 2 * 2 * (K + M) * N * J
+
+F32 = mybir.dt.float32
+BF16 = mybir.dt.bfloat16
+I32 = mybir.dt.int32
+U32 = mybir.dt.uint32
+U16 = mybir.dt.uint16
+U8 = mybir.dt.uint8
+FP8X4 = mybir.dt.float8_e4m3fn_x4
+ACT = mybir.ActivationFunctionType
+ALU = mybir.AluOpType
+
+P = 128
+PACK = 4
+NB = N // P
+JH = 512
+XC = 256
+
+
+def tile_list_tgn_ema_kernel(
+    tc, x, tab_words, tab_scales, wz_words, wz_scales, uz_words, uz_scales,
+    wn_words, wn_scales, un_words, un_scales, bz, bn, hT, wgo, offs, out,
+):
+    nc = tc.nc
+    with ExitStack() as ctx:
+        keep = ctx.enter_context(tc.tile_pool(name="keep", bufs=1))
+        ring = ctx.enter_context(tc.tile_pool(name="ring", bufs=2))
+        psum = ctx.enter_context(tc.psum_pool(name="psum", bufs=3))
+        psum1 = ctx.enter_context(tc.psum_pool(name="psum1", bufs=1))
+
+        offsets = keep.tile([P, J // 16], U16, name="offsets")
+        tabw = keep.tile([P, T], I32, name="tabw", align_bytes=64)
+        tabs = keep.tile([P, T // 4], I32, name="tabs", align_bytes=64)
+        wsc = keep.tile([P, N // 4], I32, name="wsc", align_bytes=64)
+        wq = [keep.tile([P, N], I32, name="wq%d" % w, align_bytes=64) for w in range(4)]
+        xraw = [keep.tile([P, PACK, XC], F32, name="xraw%d" % c) for c in range(J // XC)]
+        xb = [keep.tile([P, XC * PACK], BF16, name="xb%d" % c, align_bytes=64) for c in range(J // XC)]
+        xq = keep.tile([P, J], U32, name="xq", align_bytes=64)
+        xs = keep.tile([P, J], U8, name="xs", align_bytes=64)
+        vq = keep.tile([P, J], U32, name="vq", align_bytes=64)
+        vs = keep.tile([P, J], U8, name="vs", align_bytes=64)
+        hw = [keep.tile([P, T], F32, name="h%d" % b) for b in range(NB)]
+        ow = [keep.tile([P, T], F32, name="o%d" % b) for b in range(2)]
+        wg = keep.tile([P, J], F32, name="wg")
+        rows = keep.tile([P, P], F32, name="rows")
+        ident = keep.tile([P, P], F32, name="ident")
+        bias = keep.tile([P, 3 * NB], F32, name="bias")
+        warm = keep.tile([P, 1], F32, name="warm")
+
+        nc.vector.memset(tabs[:], 0)
+        nc.vector.memset(wsc[:], 0)
+        nc.vector.memset(rows[:], 0.0)
+        nc.scalar.activation(warm[:], rows[:, 0:1], ACT.Sigmoid)
+        make_identity(nc, ident[:])
+        for b in range(2):
+            nc.vector.memset(ow[b][:], 0.0)
+
+        x4 = x.rearrange("(p i) j -> p i j", i=PACK)
+        words = (wz_words, uz_words, wn_words, un_words)
+        scales = (wz_scales, uz_scales, wn_scales, un_scales)
+
+        def load_x(c):
+            nc.sync.dma_start(xraw[c][:], x4[:, :, c * XC:(c + 1) * XC])
+
+        def load_wscale(w, q):
+            nc.sync.dma_start(
+                wsc[32 * q + 4 * w:32 * q + 4 * w + 4, :], scales[w][0].bitcast(I32)[4 * q:4 * q + 4, :])
+
+        def load_w(w):
+            nc.sync.dma_start(wq[w][:], words[w][0].rearrange("p n i -> p (n i)").bitcast(I32))
+
+        def load_h(b):
+            nc.sync.dma_start(hw[b][:], hT[b * P:(b + 1) * P, :])
+
+        nc.sync.dma_start(offsets[:], offs)
+        load_x(0)
+        for q in range(4):
+            nc.sync.dma_start(tabs[32 * q:32 * q + 4, :], tab_scales[0].bitcast(I32)[4 * q:4 * q + 4, :])
+        nc.sync.dma_start(tabw[:], tab_words[0].rearrange("p t i -> p (t i)").bitcast(I32))
+        nc.sync.dma_start(rows[0:NB, :], bz.rearrange("(c p) -> c p", p=P))
+        nc.sync.dma_start(rows[NB:2 * NB, :], bn.rearrange("(c p) -> c p", p=P))
+        load_x(1)
+        for w in range(4):
+            for q in range(4):
+                load_wscale(w, q)
+            load_w(w)
+        load_h(0)
+        load_x(2)
+        load_x(3)
+        nc.sync.dma_start(wg[:], wgo)
+        for b in range(1, NB):
+            load_h(b)
+
+        bT = psum1.tile([P, P], F32, name="bT")
+        nc.tensor.transpose(bT[:], rows[:], ident[:])
+
+        def cast_x(c):
+            nc.scalar.copy(
+                xb[c][:].rearrange("p (a i t) -> p a t i", i=4, t=PACK),
+                xraw[c][:].rearrange("p t (a i) -> p a t i", i=4))
+
+        def quant_x(c):
+            cols = slice(c * XC, (c + 1) * XC)
+            nc.vector.quantize_mx(out=xq[:, cols].bitcast(FP8X4), scales=xs[:, cols], in_=xb[c][:])
+
+        def lst(h):
+            return offsets[:, h * (JH // 16):(h + 1) * (JH // 16)]
+
+        def gather_table(h):
+            cols = slice(h * JH, (h + 1) * JH)
+            nc.vector.tensor_copy(vq[:, cols], tabw[:].bitcast(U32).indirect(lst(h)))
+            nc.vector.tensor_copy(vs[:, cols], tabs[:].bitcast(U8).indirect(lst(h)))
+
+        cast_x(0)
+        cast_x(1)
+        nc.scalar.copy(bias[:, 0:2 * NB], bT[:, 0:2 * NB])
+        nc.scalar.mul(bias[:, 2 * NB:3 * NB], bT[:, 0:NB], -1.0)
+        gather_table(0)
+        quant_x(0)
+        quant_x(1)
+        gather_table(1)
+        cast_x(2)
+        cast_x(3)
+
+        wsc8 = wsc[:].bitcast(U8)
+
+        def product(b, h, w0, name):
+            cols = slice(h * JH, (h + 1) * JH)
+            ncols = slice(b * P, (b + 1) * P)
+            acc = psum.tile([P, JH], F32, name=name)
+            for i, (codes, sc) in enumerate(((xq, xs), (vq, vs))):
+                w = w0 + i
+                nc.tensor.matmul_mx(
+                    out=acc[:], lhsT=wq[w][:, ncols].bitcast(FP8X4), lhsT_scale=wsc8[4 * w:P, ncols],
+                    rhs=codes[:, cols].bitcast(FP8X4), rhs_scale=sc[:, cols], start=(i == 0), stop=(i == 1))
+            return acc
+
+        units = [(b, h) for b in range(NB) for h in range(J // JH)]
+        state = {}
+
+        def stage_a(u):
+            b, h = units[u]
+            sz = product(b, h, 0, "sz")
+            sn = product(b, h, 2, "sn")
+            y = ring.tile([P, JH], F32, name="y", bufs=3)
+            z = ring.tile([P, JH], F32, name="z", bufs=3)
+            c = ring.tile([P, JH], F32, name="c", bufs=3)
+            nc.scalar.activation(y[:], sz[:], ACT.Sigmoid, bias=bias[:, 2 * NB + b:2 * NB + b + 1], scale=-1.0)
+            nc.scalar.activation(z[:], sz[:], ACT.Sigmoid, bias=bias[:, b:b + 1])
+            nc.scalar.activation(c[:], sn[:], ACT.Tanh, bias=bias[:, NB + b:NB + b + 1])
+            state[u] = (y, z, c)
+
+        def stage_g(u):
+            b, h = units[u]
+            y, z, c = state[u]
+            g = ring.tile([P, JH], F32, name="g")
+            t = ring.tile([P, JH], F32, name="t")
+            nc.vector.tensor_tensor(t[:], z[:], c[:], ALU.mult)
+            nc.vector.tensor_tensor(g[:], hw[b][:].indirect(lst(h)), y[:], ALU.mult)
+            state[u] = (g, t)
+
+        def stage_s(u):
+            g, t = state[u]
+            s = ring.tile([P, JH], F32, name="s")
+            nc.vector.tensor_tensor(s[:], g[:], t[:], ALU.add)
+            state[u] = s
+
+        def stage_m(u):
+            b, h = units[u]
+            r = ring.tile([P, JH], F32, name="r")
+            nc.vector.tensor_tensor(r[:], state[u][:], wg[:, h * JH:(h + 1) * JH], ALU.mult)
+            state[u] = r
+
+        def stage_sc(u):
+            b, h = units[u]
+            nc.vector.tensor_copy(ow[b % 2][:].indirect(lst(h)), state[u][:])
+            if h == J // JH - 1:
+                nc.sync.dma_start(out[b * P:(b + 1) * P, :], ow[b % 2][:])
+
+        stage_a(0)
+        quant_x(2)
+        quant_x(3)
+        n_units = len(units)
+        for u in range(n_units + 1):
+            if u + 1 < n_units:
+                stage_a(u + 1)
+            if u < n_units:
+                stage_g(u)
+            if u >= 1:
+                stage_m(u - 1)
+            if u < n_units:
+                stage_s(u)
+            if u >= 1:
+                stage_sc(u - 1)

@@ -19,8 +19,11 @@ ALU = mybir.AluOpType
 P = 128
 PACK = 4
 NB = N // P
-JH = 512
 XC = 256
+HALF = J // 2
+UNITS = ((0, 0, 256), (0, 256, 512), (1, 0, 512), (0, 512, 1024), (1, 512, 1024),
+         (2, 0, 512), (2, 512, 1024), (3, 0, 512), (3, 512, 1024))
+XLOADS = ((0, 256), (256, 512), (512, 1024))
 
 
 def tile_list_tgn_ema_kernel(
@@ -30,171 +33,231 @@ def tile_list_tgn_ema_kernel(
     nc = tc.nc
     with ExitStack() as ctx:
         keep = ctx.enter_context(tc.tile_pool(name="keep", bufs=1))
-        ring = ctx.enter_context(tc.tile_pool(name="ring", bufs=2))
-        psum = ctx.enter_context(tc.psum_pool(name="psum", bufs=3))
-        psum1 = ctx.enter_context(tc.psum_pool(name="psum1", bufs=1))
+        ring = ctx.enter_context(tc.tile_pool(name="ring", bufs=3))
+        early = ctx.enter_context(tc.tile_pool(name="early", bufs=1))
+        picks = ctx.enter_context(tc.tile_pool(name="picks", bufs=4))
+        psum = ctx.enter_context(tc.psum_pool(name="psum", bufs=2))
 
         offsets = keep.tile([P, J // 16], U16, name="offsets")
         tabw = keep.tile([P, T], I32, name="tabw", align_bytes=64)
         tabs = keep.tile([P, T // 4], I32, name="tabs", align_bytes=64)
         wsc = keep.tile([P, N // 4], I32, name="wsc", align_bytes=64)
-        wq = [keep.tile([P, N], I32, name="wq%d" % w, align_bytes=64) for w in range(4)]
-        xraw = [keep.tile([P, PACK, XC], F32, name="xraw%d" % c) for c in range(J // XC)]
-        xb = [keep.tile([P, XC * PACK], BF16, name="xb%d" % c, align_bytes=64) for c in range(J // XC)]
+        wq0 = [keep.tile([P, N // 2], I32, name="wq0_%d" % w, align_bytes=64) for w in range(4)]
+        wq1 = [keep.tile([P, N // 2], I32, name="wq1_%d" % w, align_bytes=64) for w in range(4)]
+        xraw = [keep.tile([P, PACK, j1 - j0], F32, name="xraw%d" % j0) for j0, j1 in XLOADS]
+        xb = {}
         xq = keep.tile([P, J], U32, name="xq", align_bytes=64)
         xs = keep.tile([P, J], U8, name="xs", align_bytes=64)
         vq = keep.tile([P, J], U32, name="vq", align_bytes=64)
         vs = keep.tile([P, J], U8, name="vs", align_bytes=64)
         hw = [keep.tile([P, T], F32, name="h%d" % b) for b in range(NB)]
+        hg = {}
         ow = [keep.tile([P, T], F32, name="o%d" % b) for b in range(2)]
-        wg = keep.tile([P, J], F32, name="wg")
         rows = keep.tile([P, P], F32, name="rows")
         ident = keep.tile([P, P], F32, name="ident")
-        bias = keep.tile([P, 3 * NB], F32, name="bias")
+        cols16 = keep.tile([P, 16], F32, name="cols16")
         warm = keep.tile([P, 1], F32, name="warm")
 
-        nc.vector.memset(tabs[:], 0)
-        nc.vector.memset(wsc[:], 0)
-        nc.vector.memset(rows[:], 0.0)
-        nc.scalar.activation(warm[:], rows[:, 0:1], ACT.Sigmoid)
-        make_identity(nc, ident[:])
-        for b in range(2):
-            nc.vector.memset(ow[b][:], 0.0)
-
         x4 = x.rearrange("(p i) j -> p i j", i=PACK)
-        words = (wz_words, uz_words, wn_words, un_words)
-        scales = (wz_scales, uz_scales, wn_scales, un_scales)
+        words = [a[0].rearrange("p n i -> p (n i)").bitcast(I32) for a in (wz_words, uz_words, wn_words, un_words)]
+        scales = [a[0].bitcast(I32) for a in (wz_scales, uz_scales, wn_scales, un_scales)]
 
         def load_x(c):
-            nc.sync.dma_start(xraw[c][:], x4[:, :, c * XC:(c + 1) * XC])
+            nc.sync.dma_start(xraw[c][:], x4[:, :, XLOADS[c][0]:XLOADS[c][1]])
 
-        def load_wscale(w, q):
-            nc.sync.dma_start(
-                wsc[32 * q + 4 * w:32 * q + 4 * w + 4, :], scales[w][0].bitcast(I32)[4 * q:4 * q + 4, :])
+        def load_wscale(eng, w, q):
+            eng.dma_start(wsc[32 * q + 4 * w:32 * q + 4 * w + 4, :], scales[w][4 * q:4 * q + 4, :])
 
-        def load_w(w):
-            nc.sync.dma_start(wq[w][:], words[w][0].rearrange("p n i -> p (n i)").bitcast(I32))
+        def load_w0(w):
+            nc.sync.dma_start(wq0[w][:], words[w][:, 0:N // 2])
+
+        def load_w1(w):
+            nc.sync.dma_start(wq1[w][:], words[w][:, N // 2:N])
 
         def load_h(b):
             nc.sync.dma_start(hw[b][:], hT[b * P:(b + 1) * P, :])
 
-        nc.sync.dma_start(offsets[:], offs)
-        load_x(0)
-        for q in range(4):
-            nc.sync.dma_start(tabs[32 * q:32 * q + 4, :], tab_scales[0].bitcast(I32)[4 * q:4 * q + 4, :])
-        nc.sync.dma_start(tabw[:], tab_words[0].rearrange("p t i -> p (t i)").bitcast(I32))
-        nc.sync.dma_start(rows[0:NB, :], bz.rearrange("(c p) -> c p", p=P))
-        nc.sync.dma_start(rows[NB:2 * NB, :], bn.rearrange("(c p) -> c p", p=P))
-        load_x(1)
-        for w in range(4):
+        def load_tabs():
             for q in range(4):
-                load_wscale(w, q)
-            load_w(w)
-        load_h(0)
-        load_x(2)
-        load_x(3)
-        nc.sync.dma_start(wg[:], wgo)
-        for b in range(1, NB):
-            load_h(b)
+                nc.sync.dma_start(tabs[32 * q:32 * q + 4, :], tab_scales[0].bitcast(I32)[4 * q:4 * q + 4, :])
 
-        bT = psum1.tile([P, P], F32, name="bT")
-        nc.tensor.transpose(bT[:], rows[:], ident[:])
+        def load_tabw():
+            nc.sync.dma_start(tabw[:], tab_words[0].rearrange("p t i -> p (t i)").bitcast(I32))
+
+        def load_rows(i):
+            src = (bz.rearrange("(c p) -> c p", p=P), bn.rearrange("(c p) -> c p", p=P),
+                   wgo[0:1, :].rearrange("o (c p) -> (o c) p", p=P))[i]
+            dst = (rows[0:4, :], rows[4:8, :], rows[8:16, :])[i]
+            nc.sync.dma_start(dst, src)
+
+        nc.vector.memset(wsc[:], 0)
+        nc.vector.memset(tabs[:], 0)
+        nc.vector.memset(rows[:], 0.0)
+        nc.scalar.activation(warm[:], rows[:, 0:1], ACT.Sigmoid)
+        nc.vector.memset(ow[0][:, 0:T // 2 - 1], 0.0)
+        nc.vector.memset(ow[0][:, T // 2 - 1:T], 0.0)
+        make_identity(nc, ident[:])
+        planes = [(w, q) for w in (2, 3, 0, 1) for q in range(4)]
+        for w, q in planes[:10]:
+            load_wscale(nc.gpsimd, w, q)
+        nc.gpsimd.memset(ow[1][:], 0.0)
+        nc.sync.dma_start(offsets[:], offs)
+        load_tabw()
+        load_tabs()
+        load_x(0)
+        load_rows(1)
+        load_h(0)
+        load_rows(0)
+        for w in (2, 3, 0, 1):
+            load_w0(w)
+        load_x(1)
+        load_rows(2)
+        for w, q in planes[10:]:
+            load_wscale(nc.sync, w, q)
+        load_h(1)
+        load_x(2)
+        for w in (2, 3, 0, 1):
+            load_w1(w)
+        load_h(2)
+        load_h(3)
 
         def cast_x(c):
+            xb[c] = early.tile([P, XC * PACK], BF16, name="early%d" % (c % 2), align_bytes=64) if c >= 2 else keep.tile(
+                [P, XC * PACK], BF16, name="xb%d" % c, align_bytes=64)
+            src = xraw[min(c, 2)][:, :, max(c - 2, 0) * XC:(max(c - 2, 0) + 1) * XC]
             nc.scalar.copy(
                 xb[c][:].rearrange("p (a i t) -> p a t i", i=4, t=PACK),
-                xraw[c][:].rearrange("p t (a i) -> p a t i", i=4))
+                src.rearrange("p t (a i) -> p a t i", i=4))
 
         def quant_x(c):
             cols = slice(c * XC, (c + 1) * XC)
             nc.vector.quantize_mx(out=xq[:, cols].bitcast(FP8X4), scales=xs[:, cols], in_=xb[c][:])
 
-        def lst(h):
-            return offsets[:, h * (JH // 16):(h + 1) * (JH // 16)]
+        def lst(j0, j1):
+            return offsets[:, j0 // 16:j1 // 16]
 
-        def gather_table(h):
-            cols = slice(h * JH, (h + 1) * JH)
-            nc.vector.tensor_copy(vq[:, cols], tabw[:].bitcast(U32).indirect(lst(h)))
-            nc.vector.tensor_copy(vs[:, cols], tabs[:].bitcast(U8).indirect(lst(h)))
+        def gather_scales(j0, j1):
+            nc.vector.tensor_copy(vs[:, j0:j1], tabs[:].bitcast(U8).indirect(lst(j0, j1)))
 
-        cast_x(0)
-        cast_x(1)
-        nc.scalar.copy(bias[:, 0:2 * NB], bT[:, 0:2 * NB])
-        nc.scalar.mul(bias[:, 2 * NB:3 * NB], bT[:, 0:NB], -1.0)
-        gather_table(0)
-        quant_x(0)
-        quant_x(1)
-        gather_table(1)
-        cast_x(2)
-        cast_x(3)
+        def gather_words(j0, j1):
+            nc.vector.tensor_copy(vq[:, j0:j1], tabw[:].bitcast(U32).indirect(lst(j0, j1)))
+
+        def gather_h(b, j0, j1):
+            if j0 % HALF == 0:
+                hg[b, j0 // HALF] = picks.tile([P, HALF], F32, name="hg")
+            nc.vector.tensor_copy(picked(b, j0, j1), hw[b][:].indirect(lst(j0, j1)))
+
+        def picked(b, j0, j1):
+            base = j0 // HALF * HALF
+            return hg[b, j0 // HALF][:, j0 - base:j1 - base]
+
+        def small_vectors():
+            bT = psum.tile([P, 512], F32, name="sT")
+            nc.tensor.transpose(bT[:, 0:P], rows[:], ident[:])
+            nc.scalar.copy(cols16[:], bT[:, 0:16])
 
         wsc8 = wsc[:].bitcast(U8)
 
-        def product(b, h, w0, name):
-            cols = slice(h * JH, (h + 1) * JH)
-            ncols = slice(b * P, (b + 1) * P)
-            acc = psum.tile([P, JH], F32, name=name)
+        def product(b, j0, j1, w0, name):
+            acc = psum.tile([P, 512], F32, name=name)
             for i, (codes, sc) in enumerate(((xq, xs), (vq, vs))):
                 w = w0 + i
+                lhs = (wq0, wq1)[b // 2][w][:, (b % 2) * P:(b % 2 + 1) * P]
                 nc.tensor.matmul_mx(
-                    out=acc[:], lhsT=wq[w][:, ncols].bitcast(FP8X4), lhsT_scale=wsc8[4 * w:P, ncols],
-                    rhs=codes[:, cols].bitcast(FP8X4), rhs_scale=sc[:, cols], start=(i == 0), stop=(i == 1))
+                    out=acc[:, 0:j1 - j0], lhsT=lhs.bitcast(FP8X4), lhsT_scale=wsc8[4 * w:P, b * P:(b + 1) * P],
+                    rhs=codes[:, j0:j1].bitcast(FP8X4), rhs_scale=sc[:, j0:j1], start=(i == 0), stop=(i == 1))
             return acc
 
-        units = [(b, h) for b in range(NB) for h in range(J // JH)]
+        units = UNITS
         state = {}
 
-        def stage_a(u):
-            b, h = units[u]
-            sz = product(b, h, 0, "sz")
-            sn = product(b, h, 2, "sn")
-            y = ring.tile([P, JH], F32, name="y", bufs=3)
-            z = ring.tile([P, JH], F32, name="z", bufs=3)
-            c = ring.tile([P, JH], F32, name="c", bufs=3)
-            nc.scalar.activation(y[:], sz[:], ACT.Sigmoid, bias=bias[:, 2 * NB + b:2 * NB + b + 1], scale=-1.0)
-            nc.scalar.activation(z[:], sz[:], ACT.Sigmoid, bias=bias[:, b:b + 1])
-            nc.scalar.activation(c[:], sn[:], ACT.Tanh, bias=bias[:, NB + b:NB + b + 1])
-            state[u] = (y, z, c)
+        def stage_gates(u):
+            b, j0, j1 = units[u]
+            n = j1 - j0
+            sn = product(b, j0, j1, 2, "sn")
+            sz = product(b, j0, j1, 0, "sz")
+            z = ring.tile([P, 512], F32, name="z")
+            c = early.tile([P, 512], F32, name="early%d" % u, align_bytes=64) if u < 2 else ring.tile([P, 512], F32, name="c")
+            nc.scalar.activation(c[:, 0:n], sn[:, 0:n], ACT.Tanh, bias=cols16[:, NB + b:NB + b + 1])
+            nc.scalar.activation(z[:, 0:n], sz[:, 0:n], ACT.Sigmoid, bias=cols16[:, b:b + 1])
+            state[u] = (z, c)
 
-        def stage_g(u):
-            b, h = units[u]
-            y, z, c = state[u]
-            g = ring.tile([P, JH], F32, name="g")
-            t = ring.tile([P, JH], F32, name="t")
-            nc.vector.tensor_tensor(t[:], z[:], c[:], ALU.mult)
-            nc.vector.tensor_tensor(g[:], hw[b][:].indirect(lst(h)), y[:], ALU.mult)
-            state[u] = (g, t)
+        def stage_mix(u):
+            b, j0, j1 = units[u]
+            n = j1 - j0
+            z, c = state[u]
+            d = ring.tile([P, 512], F32, name="d")
+            e = ring.tile([P, 512], F32, name="e")
+            nc.gpsimd.tensor_tensor(d[:, 0:n], c[:, 0:n], picked(b, j0, j1), ALU.subtract)
+            nc.gpsimd.tensor_tensor(e[:, 0:n], z[:, 0:n], d[:, 0:n], ALU.mult)
+            state[u] = e
 
-        def stage_s(u):
-            g, t = state[u]
-            s = ring.tile([P, JH], F32, name="s")
-            nc.vector.tensor_tensor(s[:], g[:], t[:], ALU.add)
+        def stage_sum(u):
+            b, j0, j1 = units[u]
+            e = state[u]
+            sT = psum.tile([P, 512], F32, name="sT")
+            s = ring.tile([P, 512], F32, name="s")
+            for i in range((j1 - j0) // P):
+                blk = slice(i * P, (i + 1) * P)
+                nc.tensor.matmul(sT[:, blk], picked(b, j0 + i * P, j0 + (i + 1) * P), ident[:],
+                                 start=True, stop=False, is_transpose=True)
+                nc.tensor.matmul(sT[:, blk], e[:, blk], ident[:], start=False, stop=True, is_transpose=True)
+            for i in range((j1 - j0) // P):
+                blk = slice(i * P, (i + 1) * P)
+                col = 2 * NB + j0 // P + i
+                nc.scalar.activation(s[:, blk], sT[:, blk], ACT.Copy, scale=cols16[:, col:col + 1])
             state[u] = s
 
-        def stage_m(u):
-            b, h = units[u]
-            r = ring.tile([P, JH], F32, name="r")
-            nc.vector.tensor_tensor(r[:], state[u][:], wg[:, h * JH:(h + 1) * JH], ALU.mult)
+        def stage_back(u):
+            b, j0, j1 = units[u]
+            n = j1 - j0
+            s = state[u]
+            rT = psum.tile([P, 512], F32, name="rT")
+            r = ring.tile([P, 512], F32, name="r")
+            for i in range(n // P):
+                blk = slice(i * P, (i + 1) * P)
+                nc.tensor.transpose(rT[:, blk], s[:, blk], ident[:])
+            nc.scalar.copy(r[:, 0:n], rT[:, 0:n])
             state[u] = r
 
-        def stage_sc(u):
-            b, h = units[u]
-            nc.vector.tensor_copy(ow[b % 2][:].indirect(lst(h)), state[u][:])
-            if h == J // JH - 1:
+        def stage_scatter(u):
+            b, j0, j1 = units[u]
+            nc.vector.tensor_copy(ow[b % 2][:].indirect(lst(j0, j1)), state[u][:, 0:j1 - j0])
+            if j1 == J:
                 nc.sync.dma_start(out[b * P:(b + 1) * P, :], ow[b % 2][:])
 
-        stage_a(0)
-        quant_x(2)
-        quant_x(3)
+        cast_x(0)
+        cast_x(1)
+        small_vectors()
+        gather_words(0, 256)
+        gather_scales(0, 256)
+        quant_x(0)
+        gather_words(256, 512)
+        gather_scales(256, 512)
+        gather_h(0, 0, 256)
+        gather_h(0, 256, 512)
+        quant_x(1)
+        gather_words(512, 1024)
+        gather_scales(512, 1024)
+        gather_h(0, 512, 1024)
+        gather_h(1, 0, 512)
+        gather_h(1, 512, 1024)
+
         n_units = len(units)
-        for u in range(n_units + 1):
-            if u + 1 < n_units:
-                stage_a(u + 1)
+        for u in range(n_units + 4):
+            if 0 <= u - 4:
+                stage_scatter(u - 4)
+            if 0 <= u - 3 < n_units:
+                stage_back(u - 3)
+            if 0 <= u - 2 < n_units:
+                stage_sum(u - 2)
+            if 0 <= u - 1 < n_units:
+                stage_mix(u - 1)
             if u < n_units:
-                stage_g(u)
-            if u >= 1:
-                stage_m(u - 1)
-            if u < n_units:
-                stage_s(u)
-            if u >= 1:
-                stage_sc(u - 1)
+                if units[u][0] > 1:
+                    gather_h(*units[u])
+                if u == 3:
+                    for c in (2, 3):
+                        cast_x(c)
+                        quant_x(c)
+                stage_gates(u)

@@ -21,7 +21,7 @@ PACK = 4
 NB = N // P
 XC = 256
 HALF = J // 2
-UNITS = ((0, 0, 256), (0, 256, 512), (1, 0, 512), (0, 512, 1024), (1, 512, 1024),
+UNITS = ((0, 0, 256), (0, 256, 512), (0, 512, 1024), (1, 0, 512), (1, 512, 1024),
          (2, 0, 512), (2, 512, 1024), (3, 0, 512), (3, 512, 1024))
 XLOADS = ((0, 256), (256, 512), (512, 1024))
 
@@ -34,8 +34,7 @@ def tile_list_tgn_ema_kernel(
     with ExitStack() as ctx:
         keep = ctx.enter_context(tc.tile_pool(name="keep", bufs=1))
         ring = ctx.enter_context(tc.tile_pool(name="ring", bufs=3))
-        early = ctx.enter_context(tc.tile_pool(name="early", bufs=1))
-        picks = ctx.enter_context(tc.tile_pool(name="picks", bufs=4))
+        picks = ctx.enter_context(tc.tile_pool(name="picks", bufs=8))
         psum = ctx.enter_context(tc.psum_pool(name="psum", bufs=2))
 
         offsets = keep.tile([P, J // 16], U16, name="offsets")
@@ -65,8 +64,8 @@ def tile_list_tgn_ema_kernel(
         def load_x(c):
             nc.sync.dma_start(xraw[c][:], x4[:, :, XLOADS[c][0]:XLOADS[c][1]])
 
-        def load_wscale(eng, w, q):
-            eng.dma_start(wsc[32 * q + 4 * w:32 * q + 4 * w + 4, :], scales[w][4 * q:4 * q + 4, :])
+        def load_wscale(w, q):
+            nc.sync.dma_start(wsc[32 * q + 4 * w:32 * q + 4 * w + 4, :], scales[w][4 * q:4 * q + 4, :])
 
         def load_w0(w):
             nc.sync.dma_start(wq0[w][:], words[w][:, 0:N // 2])
@@ -77,9 +76,8 @@ def tile_list_tgn_ema_kernel(
         def load_h(b):
             nc.sync.dma_start(hw[b][:], hT[b * P:(b + 1) * P, :])
 
-        def load_tabs():
-            for q in range(4):
-                nc.sync.dma_start(tabs[32 * q:32 * q + 4, :], tab_scales[0].bitcast(I32)[4 * q:4 * q + 4, :])
+        def load_tabs(q):
+            nc.sync.dma_start(tabs[32 * q:32 * q + 4, :], tab_scales[0].bitcast(I32)[4 * q:4 * q + 4, :])
 
         def load_tabw():
             nc.sync.dma_start(tabw[:], tab_words[0].rearrange("p t i -> p (t i)").bitcast(I32))
@@ -90,40 +88,35 @@ def tile_list_tgn_ema_kernel(
             dst = (rows[0:4, :], rows[4:8, :], rows[8:16, :])[i]
             nc.sync.dma_start(dst, src)
 
-        nc.vector.memset(wsc[:], 0)
-        nc.vector.memset(tabs[:], 0)
+        nc.gpsimd.memset(tabs[:], 0)
         nc.vector.memset(rows[:], 0.0)
+        nc.vector.memset(wsc[:], 0)
         nc.scalar.activation(warm[:], rows[:, 0:1], ACT.Sigmoid)
-        nc.vector.memset(ow[0][:, 0:T // 2 - 1], 0.0)
-        nc.vector.memset(ow[0][:, T // 2 - 1:T], 0.0)
+        nc.vector.memset(ow[0][:], 0.0)
         make_identity(nc, ident[:])
-        planes = [(w, q) for w in (2, 3, 0, 1) for q in range(4)]
-        for w, q in planes[:10]:
-            load_wscale(nc.gpsimd, w, q)
         nc.gpsimd.memset(ow[1][:], 0.0)
-        nc.sync.dma_start(offsets[:], offs)
-        load_tabw()
-        load_tabs()
-        load_x(0)
-        load_rows(1)
-        load_h(0)
-        load_rows(0)
-        for w in (2, 3, 0, 1):
-            load_w0(w)
-        load_x(1)
-        load_rows(2)
-        for w, q in planes[10:]:
-            load_wscale(nc.sync, w, q)
-        load_h(1)
-        load_x(2)
-        for w in (2, 3, 0, 1):
-            load_w1(w)
-        load_h(2)
-        load_h(3)
+        small = [lambda: nc.sync.dma_start(offsets[:], offs)]
+        small += [lambda q=q: load_tabs(q) for q in range(4)]
+        small += [lambda i=i: load_rows(i) for i in range(3)]
+        small += [lambda w=w, q=q: load_wscale(w, q) for w in (2, 3, 0, 1) for q in range(4)]
+        big = {"T": load_tabw}
+        for i in range(4):
+            big["w%d" % i] = lambda i=i: load_w0(i)
+            big["v%d" % i] = lambda i=i: load_w1(i)
+            big["h%d" % i] = lambda i=i: load_h(i)
+        for i in range(3):
+            big["x%d" % i] = lambda i=i: load_x(i)
+        k = 0
+        for item in "w2 w3 w0 s w1 T s s s s s s h0 s x0 s s x1 s s s x2 s s s s s h1 s s s s s s h2 h3 v2 v3 v0 v1".split():
+            if item == "s":
+                small[k]()
+                k += 1
+            else:
+                big[item]()
+        assert k == len(small)
 
         def cast_x(c):
-            xb[c] = early.tile([P, XC * PACK], BF16, name="early%d" % (c % 2), align_bytes=64) if c >= 2 else keep.tile(
-                [P, XC * PACK], BF16, name="xb%d" % c, align_bytes=64)
+            xb[c] = keep.tile([P, XC * PACK], BF16, name="xb%d" % c, align_bytes=64)
             src = xraw[min(c, 2)][:, :, max(c - 2, 0) * XC:(max(c - 2, 0) + 1) * XC]
             nc.scalar.copy(
                 xb[c][:].rearrange("p (a i t) -> p a t i", i=4, t=PACK),
@@ -177,7 +170,7 @@ def tile_list_tgn_ema_kernel(
             sn = product(b, j0, j1, 2, "sn")
             sz = product(b, j0, j1, 0, "sz")
             z = ring.tile([P, 512], F32, name="z")
-            c = early.tile([P, 512], F32, name="early%d" % u, align_bytes=64) if u < 2 else ring.tile([P, 512], F32, name="c")
+            c = ring.tile([P, 512], F32, name="c")
             nc.scalar.activation(c[:, 0:n], sn[:, 0:n], ACT.Tanh, bias=cols16[:, NB + b:NB + b + 1])
             nc.scalar.activation(z[:, 0:n], sz[:, 0:n], ACT.Sigmoid, bias=cols16[:, b:b + 1])
             state[u] = (z, c)
@@ -240,6 +233,9 @@ def tile_list_tgn_ema_kernel(
         gather_words(512, 1024)
         gather_scales(512, 1024)
         gather_h(0, 512, 1024)
+        for c in (2, 3):
+            cast_x(c)
+            quant_x(c)
         gather_h(1, 0, 512)
         gather_h(1, 512, 1024)
 
@@ -256,8 +252,4 @@ def tile_list_tgn_ema_kernel(
             if u < n_units:
                 if units[u][0] > 1:
                     gather_h(*units[u])
-                if u == 3:
-                    for c in (2, 3):
-                        cast_x(c)
-                        quant_x(c)
                 stage_gates(u)

from contextlib import ExitStack

import concourse.mybir as mybir
from concourse.masks import make_identity

K, M, N, T, J = 512, 512, 512, 2048, 1024
FLOPS = 2 * 2 * (K + M) * N * J

F32 = mybir.dt.float32
BF16 = mybir.dt.bfloat16
I32 = mybir.dt.int32
U32 = mybir.dt.uint32
U16 = mybir.dt.uint16
U8 = mybir.dt.uint8
FP8X4 = mybir.dt.float8_e4m3fn_x4
ACT = mybir.ActivationFunctionType
ALU = mybir.AluOpType

P = 128
PACK = 4
NB = N // P
XC = 256
HALF = J // 2
UNITS = ((0, 0, 256), (0, 256, 512), (0, 512, 1024), (1, 0, 512), (1, 512, 1024),
         (2, 0, 512), (2, 512, 1024), (3, 0, 512), (3, 512, 1024))
XLOADS = ((0, 256), (256, 512), (512, 1024))


def tile_list_tgn_ema_kernel(
    tc, x, tab_words, tab_scales, wz_words, wz_scales, uz_words, uz_scales,
    wn_words, wn_scales, un_words, un_scales, bz, bn, hT, wgo, offs, out,
):
    nc = tc.nc
    with ExitStack() as ctx:
        keep = ctx.enter_context(tc.tile_pool(name="keep", bufs=1))
        ring = ctx.enter_context(tc.tile_pool(name="ring", bufs=3))
        picks = ctx.enter_context(tc.tile_pool(name="picks", bufs=8))
        psum = ctx.enter_context(tc.psum_pool(name="psum", bufs=2))

        offsets = keep.tile([P, J // 16], U16, name="offsets")
        tabw = keep.tile([P, T], I32, name="tabw", align_bytes=64)
        tabs = keep.tile([P, T // 4], I32, name="tabs", align_bytes=64)
        wsc = keep.tile([P, N // 4], I32, name="wsc", align_bytes=64)
        wq0 = [keep.tile([P, N // 2], I32, name="wq0_%d" % w, align_bytes=64) for w in range(4)]
        wq1 = [keep.tile([P, N // 2], I32, name="wq1_%d" % w, align_bytes=64) for w in range(4)]
        xraw = [keep.tile([P, PACK, j1 - j0], F32, name="xraw%d" % j0) for j0, j1 in XLOADS]
        xb = {}
        xq = keep.tile([P, J], U32, name="xq", align_bytes=64)
        xs = keep.tile([P, J], U8, name="xs", align_bytes=64)
        vq = keep.tile([P, J], U32, name="vq", align_bytes=64)
        vs = keep.tile([P, J], U8, name="vs", align_bytes=64)
        hw = [keep.tile([P, T], F32, name="h%d" % b) for b in range(NB)]
        hg = {}
        ow = [keep.tile([P, T], F32, name="o%d" % b) for b in range(2)]
        rows = keep.tile([P, P], F32, name="rows")
        ident = keep.tile([P, P], F32, name="ident")
        cols16 = keep.tile([P, 16], F32, name="cols16")
        warm = keep.tile([P, 1], F32, name="warm")

        x4 = x.rearrange("(p i) j -> p i j", i=PACK)
        words = [a[0].rearrange("p n i -> p (n i)").bitcast(I32) for a in (wz_words, uz_words, wn_words, un_words)]
        scales = [a[0].bitcast(I32) for a in (wz_scales, uz_scales, wn_scales, un_scales)]

        def load_x(c):
            nc.sync.dma_start(xraw[c][:], x4[:, :, XLOADS[c][0]:XLOADS[c][1]])

        def load_wscale(w, q):
            nc.sync.dma_start(wsc[32 * q + 4 * w:32 * q + 4 * w + 4, :], scales[w][4 * q:4 * q + 4, :])

        def load_w0(w):
            nc.sync.dma_start(wq0[w][:], words[w][:, 0:N // 2])

        def load_w1(w):
            nc.sync.dma_start(wq1[w][:], words[w][:, N // 2:N])

        def load_h(b):
            nc.sync.dma_start(hw[b][:], hT[b * P:(b + 1) * P, :])

        def load_tabs(q):
            nc.sync.dma_start(tabs[32 * q:32 * q + 4, :], tab_scales[0].bitcast(I32)[4 * q:4 * q + 4, :])

        def load_tabw():
            nc.sync.dma_start(tabw[:], tab_words[0].rearrange("p t i -> p (t i)").bitcast(I32))

        def load_rows(i):
            src = (bz.rearrange("(c p) -> c p", p=P), bn.rearrange("(c p) -> c p", p=P),
                   wgo[0:1, :].rearrange("o (c p) -> (o c) p", p=P))[i]
            dst = (rows[0:4, :], rows[4:8, :], rows[8:16, :])[i]
            nc.sync.dma_start(dst, src)

        nc.gpsimd.memset(tabs[:], 0)
        nc.vector.memset(rows[:], 0.0)
        nc.vector.memset(wsc[:], 0)
        nc.scalar.activation(warm[:], rows[:, 0:1], ACT.Sigmoid)
        nc.vector.memset(ow[0][:], 0.0)
        make_identity(nc, ident[:])
        nc.gpsimd.memset(ow[1][:], 0.0)
        small = [lambda: nc.sync.dma_start(offsets[:], offs)]
        small += [lambda q=q: load_tabs(q) for q in range(4)]
        small += [lambda i=i: load_rows(i) for i in range(3)]
        small += [lambda w=w, q=q: load_wscale(w, q) for w in (2, 3, 0, 1) for q in range(4)]
        big = {"T": load_tabw}
        for i in range(4):
            big["w%d" % i] = lambda i=i: load_w0(i)
            big["v%d" % i] = lambda i=i: load_w1(i)
            big["h%d" % i] = lambda i=i: load_h(i)
        for i in range(3):
            big["x%d" % i] = lambda i=i: load_x(i)
        k = 0
        for item in "w2 w3 w0 s w1 T s s s s s s h0 s x0 s s x1 s s s x2 s s s s s h1 s s s s s s h2 h3 v2 v3 v0 v1".split():
            if item == "s":
                small[k]()
                k += 1
            else:
                big[item]()
        assert k == len(small)

        def cast_x(c):
            xb[c] = keep.tile([P, XC * PACK], BF16, name="xb%d" % c, align_bytes=64)
            src = xraw[min(c, 2)][:, :, max(c - 2, 0) * XC:(max(c - 2, 0) + 1) * XC]
            nc.scalar.copy(
                xb[c][:].rearrange("p (a i t) -> p a t i", i=4, t=PACK),
                src.rearrange("p t (a i) -> p a t i", i=4))

        def quant_x(c):
            cols = slice(c * XC, (c + 1) * XC)
            nc.vector.quantize_mx(out=xq[:, cols].bitcast(FP8X4), scales=xs[:, cols], in_=xb[c][:])

        def lst(j0, j1):
            return offsets[:, j0 // 16:j1 // 16]

        def gather_scales(j0, j1):
            nc.vector.tensor_copy(vs[:, j0:j1], tabs[:].bitcast(U8).indirect(lst(j0, j1)))

        def gather_words(j0, j1):
            nc.vector.tensor_copy(vq[:, j0:j1], tabw[:].bitcast(U32).indirect(lst(j0, j1)))

        def gather_h(b, j0, j1):
            if j0 % HALF == 0:
                hg[b, j0 // HALF] = picks.tile([P, HALF], F32, name="hg")
            nc.vector.tensor_copy(picked(b, j0, j1), hw[b][:].indirect(lst(j0, j1)))

        def picked(b, j0, j1):
            base = j0 // HALF * HALF
            return hg[b, j0 // HALF][:, j0 - base:j1 - base]

        def small_vectors():
            bT = psum.tile([P, 512], F32, name="sT")
            nc.tensor.transpose(bT[:, 0:P], rows[:], ident[:])
            nc.scalar.copy(cols16[:], bT[:, 0:16])

        wsc8 = wsc[:].bitcast(U8)

        def product(b, j0, j1, w0, name):
            acc = psum.tile([P, 512], F32, name=name)
            for i, (codes, sc) in enumerate(((xq, xs), (vq, vs))):
                w = w0 + i
                lhs = (wq0, wq1)[b // 2][w][:, (b % 2) * P:(b % 2 + 1) * P]
                nc.tensor.matmul_mx(
                    out=acc[:, 0:j1 - j0], lhsT=lhs.bitcast(FP8X4), lhsT_scale=wsc8[4 * w:P, b * P:(b + 1) * P],
                    rhs=codes[:, j0:j1].bitcast(FP8X4), rhs_scale=sc[:, j0:j1], start=(i == 0), stop=(i == 1))
            return acc

        units = UNITS
        state = {}

        def stage_gates(u):
            b, j0, j1 = units[u]
            n = j1 - j0
            sn = product(b, j0, j1, 2, "sn")
            sz = product(b, j0, j1, 0, "sz")
            z = ring.tile([P, 512], F32, name="z")
            c = ring.tile([P, 512], F32, name="c")
            nc.scalar.activation(c[:, 0:n], sn[:, 0:n], ACT.Tanh, bias=cols16[:, NB + b:NB + b + 1])
            nc.scalar.activation(z[:, 0:n], sz[:, 0:n], ACT.Sigmoid, bias=cols16[:, b:b + 1])
            state[u] = (z, c)

        def stage_mix(u):
            b, j0, j1 = units[u]
            n = j1 - j0
            z, c = state[u]
            d = ring.tile([P, 512], F32, name="d")
            e = ring.tile([P, 512], F32, name="e")
            nc.gpsimd.tensor_tensor(d[:, 0:n], c[:, 0:n], picked(b, j0, j1), ALU.subtract)
            nc.gpsimd.tensor_tensor(e[:, 0:n], z[:, 0:n], d[:, 0:n], ALU.mult)
            state[u] = e

        def stage_sum(u):
            b, j0, j1 = units[u]
            e = state[u]
            sT = psum.tile([P, 512], F32, name="sT")
            s = ring.tile([P, 512], F32, name="s")
            for i in range((j1 - j0) // P):
                blk = slice(i * P, (i + 1) * P)
                nc.tensor.matmul(sT[:, blk], picked(b, j0 + i * P, j0 + (i + 1) * P), ident[:],
                                 start=True, stop=False, is_transpose=True)
                nc.tensor.matmul(sT[:, blk], e[:, blk], ident[:], start=False, stop=True, is_transpose=True)
            for i in range((j1 - j0) // P):
                blk = slice(i * P, (i + 1) * P)
                col = 2 * NB + j0 // P + i
                nc.scalar.activation(s[:, blk], sT[:, blk], ACT.Copy, scale=cols16[:, col:col + 1])
            state[u] = s

        def stage_back(u):
            b, j0, j1 = units[u]
            n = j1 - j0
            s = state[u]
            rT = psum.tile([P, 512], F32, name="rT")
            r = ring.tile([P, 512], F32, name="r")
            for i in range(n // P):
                blk = slice(i * P, (i + 1) * P)
                nc.tensor.transpose(rT[:, blk], s[:, blk], ident[:])
            nc.scalar.copy(r[:, 0:n], rT[:, 0:n])
            state[u] = r

        def stage_scatter(u):
            b, j0, j1 = units[u]
            nc.vector.tensor_copy(ow[b % 2][:].indirect(lst(j0, j1)), state[u][:, 0:j1 - j0])
            if j1 == J:
                nc.sync.dma_start(out[b * P:(b + 1) * P, :], ow[b % 2][:])

        cast_x(0)
        cast_x(1)
        small_vectors()
        gather_words(0, 256)
        gather_scales(0, 256)
        quant_x(0)
        gather_words(256, 512)
        gather_scales(256, 512)
        gather_h(0, 0, 256)
        gather_h(0, 256, 512)
        quant_x(1)
        gather_words(512, 1024)
        gather_scales(512, 1024)
        gather_h(0, 512, 1024)
        for c in (2, 3):
            cast_x(c)
            quant_x(c)
        gather_h(1, 0, 512)
        gather_h(1, 512, 1024)

        n_units = len(units)
        for u in range(n_units + 4):
            if 0 <= u - 4:
                stage_scatter(u - 4)
            if 0 <= u - 3 < n_units:
                stage_back(u - 3)
            if 0 <= u - 2 < n_units:
                stage_sum(u - 2)
            if 0 <= u - 1 < n_units:
                stage_mix(u - 1)
            if u < n_units:
                if units[u][0] > 1:
                    gather_h(*units[u])
                stage_gates(u)
